import numpy as np
import ml_dtypes


def mxq(x, axis, fmt="e4m3"):
    dtype, down = {"e4m3": (ml_dtypes.float8_e4m3fn, 7), "e5m2": (ml_dtypes.float8_e5m2, 14)}[fmt]
    v = np.moveaxis(np.asarray(x, np.float32).astype(ml_dtypes.bfloat16).astype(np.float64), axis, -1)
    blocks = v.reshape(v.shape[:-1] + (-1, 32))
    amax = np.abs(blocks).max(-1, keepdims=True)
    byte = np.maximum(np.where(amax > 0, np.frexp(amax)[1] - 1 + 127, 0) - down, 1)
    scale = np.exp2(byte - 127.0)
    codes = (blocks / scale).astype(np.float32).astype(dtype).astype(np.float64)
    return np.moveaxis((codes * scale).reshape(v.shape), -1, axis)


WIDE = False


def mx_kscale(k):
    if not WIDE:
        return np.ones(k)
    levels = np.array([10, -10, 5, -5, 0])
    if k % 512:
        return np.exp2(np.random.permutation(np.resize(levels, k // 32))).repeat(32)
    a = np.empty((k // 512, 16))
    for p in range(k // 512):
        a[p, :8] = np.random.permutation(np.resize(levels, 8))
        for g in range(8):
            far = levels[np.abs(levels - a[p, g]) >= 10]
            a[p, g + 8] = far[np.random.randint(len(far))]
    return np.exp2(a.ravel()).repeat(32)


def f64(x):
    return np.asarray(x).astype(np.float64)


def striped(idx):
    return np.tile(idx.reshape(-1, 16).T, (8, 1)).astype(np.uint16)


def unstriped(offs):
    return offs[:16].T.reshape(-1).astype(np.int64)


def striped8(idx):
    return np.concatenate([x.reshape(-1, 16).T for x in idx]).astype(np.uint16)


def runs(offs, k):
    lists = np.stack([offs[16 * r : 16 * r + 16].T.reshape(-1) for r in range(8)]).astype(np.int64)
    return lists[np.arange(k) % 512 // 64]


def pack_weight(w):
    k, n = w.shape
    w = f64(np.asarray(w, np.float32).astype(ml_dtypes.bfloat16)).reshape(k // 32, 32, n)
    amax = np.abs(w).max(1)
    byte = np.clip(np.where(amax > 0, np.frexp(amax)[1] - 1 + 127 - 7, 1), 1, 254)
    scaled = (w * np.exp2(127.0 - byte)[:, None, :]).reshape(k, n).astype(np.float32)
    words = np.ascontiguousarray(scaled.reshape(k // 512, 128, 4, n).transpose(0, 1, 3, 2)).astype(ml_dtypes.float8_e4m3fn).view(np.uint8)
    return words, np.ascontiguousarray(byte.astype(np.uint8).reshape(k // 512, 16, n))


def unpack_weight(words, scales):
    g, p, n, _ = words.shape
    vals = np.ascontiguousarray(words).view(ml_dtypes.float8_e4m3fn).astype(np.float64) * np.repeat(np.exp2(scales.astype(np.float64) - 127.0), 8, axis=1)[..., None]
    return vals.transpose(0, 1, 3, 2).reshape(g * 512, n)


E2M1 = np.array([0.0, 0.5, 1.0, 1.5, 2.0, 3.0, 4.0, 6.0, -0.0, -0.5, -1.0, -1.5, -2.0, -3.0, -4.0, -6.0])


def pack_fp4(w):
    k, n = w.shape
    w = f64(np.asarray(w, np.float32).astype(ml_dtypes.bfloat16)).reshape(k // 32, 32, n)
    amax = np.abs(w).max(1)
    mant, ex = np.frexp(amax / 6.0)
    byte = np.clip(np.where(amax > 0, np.where(mant > 0.5, ex, ex - 1) + 127, 1), 1, 254)
    scaled = (w * np.exp2(127.0 - byte)[:, None, :]).reshape(k, n).astype(np.float32)
    c = np.ascontiguousarray(scaled.reshape(k // 512, 128, 4, n).transpose(0, 1, 3, 2)).astype(ml_dtypes.float4_e2m1fn).view(np.uint8) & 0xF
    words = (c[..., 0::2] | (c[..., 1::2] << 4)).reshape(k // 512, 128, 2 * n)
    return np.ascontiguousarray(words), np.ascontiguousarray(byte.astype(np.uint8).reshape(k // 512, 16, n))


def unpack_fp4(words, scales):
    g, _, n = scales.shape
    words = np.ascontiguousarray(words).reshape(g, 128, n, 2)
    nib = np.empty((g, 128, n, 4), np.uint8)
    nib[..., 0::2] = words & 0xF
    nib[..., 1::2] = words >> 4
    vals = E2M1[nib] * np.repeat(np.exp2(scales.astype(np.float64) - 127.0), 8, axis=1)[..., None]
    return vals.transpose(0, 1, 3, 2).reshape(g * 512, n)


K, T, S, H, C, W = 512, 2048, 512, 512, 512, 256


def setup_inputs():
    n = np.random.standard_normal
    s = mx_kscale(K)[:, None]
    packed_xT = pack_weight(n((K, T)) * s)
    packed_w1 = pack_fp4(n((K, H)) / np.sqrt(2 * K) / s)
    packed_w2 = pack_fp4(n((K, H)) / np.sqrt(2 * K) / s)
    perm = np.stack([np.random.permutation(S) for _ in range(8)])
    return {
        "x_words": packed_xT[0],
        "x_scales": packed_xT[1],
        "w1_words": packed_w1[0],
        "w1_scales": packed_w1[1],
        "w2_words": packed_w2[0],
        "w2_scales": packed_w2[1],
        "gs": (np.random.uniform(0.5, 1.5, (K, 1)) / s).astype(np.float32),
        "offs": striped(np.random.permutation(T)[:S]),
        "hz": striped8(np.random.randint(0, T, (8, S))),
        "cand": striped(np.random.permutation(T)[:C]),
        "n1": striped8(perm[:, :W]),
        "n2": striped8(perm[:, W:]),
    }


def reference(x_words, x_scales, w1_words, w1_scales, w2_words, w2_scales, gs, offs, hz, cand, n1, n2):
    x_cand = unpack_weight(x_words, x_scales)[:, unstriped(cand)]
    xq = unpack_weight(x_words, x_scales)[:, unstriped(offs)]
    x_hz = unpack_weight(x_words, x_scales)[np.arange(K)[:, None], runs(hz, K)]
    y = unpack_fp4(w1_words, w1_scales).T @ xq + unpack_fp4(w2_words, w2_scales).T @ x_hz
    z = f64(gs) * y
    s = 0.0625 * ((x_cand.T @ mxq(z, 0, "e4m3")))
    pa = s[np.arange(C)[:, None], runs(n1, C)]
    pb = s[np.arange(C)[:, None], runs(n2, C)]
    ra = np.maximum(pa, pb)
    out = s.copy()
    out[np.arange(C)[:, None], runs(n1, C)] = ra
    return out

@@ -1,0 +1,151 @@
+from contextlib import ExitStack
+
+import concourse.mybir as mybir
+
+K, T, S, H, C, W = 512, 2048, 512, 512, 512, 256
+FLOPS = 3 * 2 * 512 * 512 * 512
+
+F32 = mybir.dt.float32
+BF16 = mybir.dt.bfloat16
+I32 = mybir.dt.int32
+U32 = mybir.dt.uint32
+U16 = mybir.dt.uint16
+U8 = mybir.dt.uint8
+FP8X4 = mybir.dt.float8_e4m3fn_x4
+FP4X4 = mybir.dt.float4_e2m1fn_x4
+COPY = mybir.ActivationFunctionType.Copy
+MAX = mybir.AluOpType.max
+
+P = 128
+PACK = 4
+HALF = S // 2
+QUAD = 32
+
+
+def tile_picked_thcifill_none_p_kernel(
+    tc, x_words, x_scales, w1_words, w1_scales, w2_words, w2_scales, gs, offs, hz, cand, n1, n2, out
+):
+    nc = tc.nc
+    with ExitStack() as ctx:
+        lists = ctx.enter_context(tc.tile_pool(name="lists", bufs=1))
+        sb = ctx.enter_context(tc.tile_pool(name="sb", bufs=1))
+        psum = ctx.enter_context(tc.psum_pool(name="psum", bufs=1))
+
+        hz_l = lists.tile([P, S // 16], U16, name="hz_l")
+        offs_l = lists.tile([P, S // 16], U16, name="offs_l")
+        cand_l = lists.tile([P, C // 16], U16, name="cand_l")
+        n1_l = lists.tile([P, W // 16], U16, name="n1_l")
+        n2_l = lists.tile([P, W // 16], U16, name="n2_l")
+        for dst, src in ((hz_l, hz), (offs_l, offs), (cand_l, cand), (n1_l, n1), (n2_l, n2)):
+            nc.sync.dma_start(dst[:], src)
+
+        xw = sb.tile([P, T], U32, name="xw", align_bytes=64)
+        nc.gpsimd.dma_start(xw[:].bitcast(I32), x_words[0].rearrange("p n t -> p (n t)").bitcast(I32))
+        w_raw = [sb.tile([P, 2 * H], U8, name="w_raw%d" % a, align_bytes=64) for a in range(2)]
+        for a, words in enumerate((w1_words, w2_words)):
+            nc.gpsimd.dma_start(w_raw[a][:].bitcast(I32), words[0].bitcast(I32))
+        gain = sb.tile([P, PACK], F32, name="gain")
+        nc.gpsimd.dma_start(gain[:], gs.rearrange("(p t) o -> p (t o)", t=PACK))
+
+        x_rows = x_scales[0].bitcast(I32)
+        xs_run = sb.tile([P, T], U8, name="xs_run", align_bytes=64)
+        nc.vector.memset(xs_run[:].bitcast(I32), 0)
+        nc.scalar.dma_start(xs_run[0:P:8, :].bitcast(I32), x_rows)
+        xs = sb.tile([P, T], U8, name="xs", align_bytes=64)
+        nc.vector.memset(xs[:].bitcast(I32), 0)
+        for i in range(PACK):
+            nc.scalar.dma_start(xs[i:P:QUAD, :].bitcast(I32), x_rows[i:16:PACK, :])
+        ws_raw = [sb.tile([P, H], U8, name="ws_raw%d" % a, align_bytes=64) for a in range(2)]
+        for a, scales in enumerate((w1_scales, w2_scales)):
+            nc.vector.memset(ws_raw[a][:].bitcast(I32), 0)
+            rows = scales[0].bitcast(I32)
+            for i in range(PACK):
+                nc.scalar.dma_start(ws_raw[a][i:P:QUAD, :].bitcast(I32), rows[i:16:PACK, :])
+
+        hz_run = sb.tile([P, S], U8, name="hz_run", align_bytes=64)
+        nc.vector.tensor_copy(hz_run[:], xs_run[:].indirect(hz_l[:]))
+        hz_s = sb.tile([P, S], U8, name="hz_s", align_bytes=64)
+        nc.vector.memset(hz_s[:].bitcast(I32), 0)
+        for i in range(PACK):
+            nc.scalar.dma_start(hz_s[i:P:QUAD, :].bitcast(I32), hz_run[8 * i : P : QUAD, :].bitcast(I32))
+        tok_s = sb.tile([P, S], U8, name="tok_s", align_bytes=64)
+        nc.vector.tensor_copy(tok_s[:], xs[:].indirect(offs_l[:]))
+
+        w = [sb.tile([P, 2 * H], U8, name="w%d" % a, align_bytes=64) for a in range(2)]
+        ws = [sb.tile([P, H], U8, name="ws%d" % a, align_bytes=64) for a in range(2)]
+        for a in range(2):
+            nc.scalar.copy(
+                w[a][:].bitcast(U16).rearrange("p (t m) -> p t m", t=PACK),
+                w_raw[a][:].bitcast(U16).rearrange("p (m t) -> p t m", t=PACK),
+            )
+            nc.vector.tensor_copy(
+                ws[a][:].rearrange("p (t m) -> p t m", t=PACK),
+                ws_raw[a][:].rearrange("p (m t) -> p t m", t=PACK),
+            )
+
+        tok_w = [sb.tile([P, HALF], U32, name="tok_w%d" % h, align_bytes=64) for h in range(2)]
+        hz_w = [sb.tile([P, HALF], U32, name="hz_w%d" % h, align_bytes=64) for h in range(2)]
+        z_rows = [sb.tile([P, PACK, HALF], BF16, name="z_rows%d" % h, align_bytes=64) for h in range(2)]
+        for h in range(2):
+            entries = slice(h * HALF // 16, (h + 1) * HALF // 16)
+            cols = slice(h * HALF, (h + 1) * HALF)
+            nc.vector.tensor_copy(tok_w[h][:], xw[:].indirect(offs_l[:, entries]))
+            nc.vector.tensor_copy(hz_w[h][:], xw[:].indirect(hz_l[:, entries]))
+            y = [psum.tile([P, HALF], F32, name="y%d%d" % (t, h), tag="bank%d%d" % (t, h)) for t in range(PACK)]
+            for a, (words, scales) in enumerate(((tok_w[h], tok_s), (hz_w[h], hz_s))):
+                for t in range(PACK):
+                    nc.tensor.matmul_mx(
+                        out=y[t][:],
+                        lhsT=w[a][:, 2 * P * t : 2 * P * (t + 1)].bitcast(FP4X4),
+                        lhsT_scale=ws[a][:, P * t : P * (t + 1)],
+                        rhs=words[:].bitcast(FP8X4),
+                        rhs_scale=scales[:, cols],
+                        start=(a == 0),
+                        stop=(a == 1),
+                    )
+            for t in range(PACK):
+                nc.scalar.activation(z_rows[h][:, t, :], y[t][:], COPY, scale=gain[:, t : t + 1])
+
+        cand_s = sb.tile([P, C], U8, name="cand_s", align_bytes=64)
+        nc.vector.tensor_copy(cand_s[:].rearrange("p (t m) -> p m t", t=PACK), xs[:].indirect(cand_l[:]))
+        cand_w = sb.tile([P, C], U32, name="cand_w", align_bytes=64)
+        nc.vector.tensor_copy(cand_w[:].rearrange("p (t m) -> p m t", t=PACK), xw[:].indirect(cand_l[:]))
+
+        s = [sb.tile([P, S], F32, name="s%d" % t, align_bytes=64) for t in range(PACK)]
+        acc = {}
+        for h in range(2):
+            z = sb.tile([P, HALF, PACK], BF16, name="z%d" % h, align_bytes=64)
+            nc.vector.tensor_copy(
+                z[:].rearrange("p (c i) t -> p c t i", i=PACK),
+                z_rows[h][:].rearrange("p t (c i) -> p c t i", i=PACK),
+            )
+            z_w = sb.tile([P, HALF], U32, name="z_w%d" % h, align_bytes=64)
+            z_s = sb.tile([P, HALF], U8, name="z_s%d" % h, align_bytes=64)
+            nc.vector.quantize_mx(out=z_w[:].bitcast(FP8X4), scales=z_s[:], in_=z[:].rearrange("p j t -> p (j t)"))
+            for t in range(PACK):
+                acc[t, h] = psum.tile([P, HALF], F32, name="acc%d%d" % (t, h), tag="bank%d%d" % (t, h))
+                nc.tensor.matmul_mx(
+                    out=acc[t, h][:],
+                    lhsT=cand_w[:, P * t : P * (t + 1)].bitcast(FP8X4),
+                    lhsT_scale=cand_s[:, P * t : P * (t + 1)],
+                    rhs=z_w[:].bitcast(FP8X4),
+                    rhs_scale=z_s[:],
+                    start=True,
+                    stop=True,
+                )
+
+        out_rows = out.rearrange("(p t) j -> p t j", t=PACK)
+        for t in range(PACK):
+            for h in range(2):
+                nc.scalar.activation(s[t][:, h * HALF : (h + 1) * HALF], acc[t, h][:], COPY, scale=0.0625)
+            pa = sb.tile([P, W], F32, name="pa%d" % t, align_bytes=64)
+            pb = sb.tile([P, W], F32, name="pb%d" % t, align_bytes=64)
+            ra = sb.tile([P, W], F32, name="ra%d" % t, align_bytes=64)
+            nc.scalar.activation(pb[:], s[t][:].indirect(n2_l[:]), COPY)
+            if t == 0:
+                nc.vector.tensor_copy(pa[:], s[t][:].indirect(n1_l[:]))
+            else:
+                nc.scalar.activation(pa[:], s[t][:].indirect(n1_l[:]), COPY)
+            nc.vector.tensor_tensor(ra[:], pa[:], pb[:], MAX)
+            nc.vector.tensor_copy(s[t][:].indirect(n1_l[:]), ra[:])
+            nc.sync.dma_start(out_rows[:, t, :], s[t][:])

@@ -36,13 +36,13 @@ def tile_picked_thcifill_none_p_kernel(
         cand_l = lists.tile([P, C // 16], U16, name="cand_l")
         n1_l = lists.tile([P, W // 16], U16, name="n1_l")
         n2_l = lists.tile([P, W // 16], U16, name="n2_l")
-        for dst, src in ((hz_l, hz), (offs_l, offs), (cand_l, cand), (n1_l, n1), (n2_l, n2)):
+        for dst, src in ((hz_l, hz), (offs_l, offs)):
             nc.sync.dma_start(dst[:], src)
 
         xw = sb.tile([P, T], U32, name="xw", align_bytes=64)
-        nc.gpsimd.dma_start(xw[:].bitcast(I32), x_words[0].rearrange("p n t -> p (n t)").bitcast(I32))
+        nc.sync.dma_start(xw[:].bitcast(I32), x_words[0].rearrange("p n t -> p (n t)").bitcast(I32))
         w_raw = [sb.tile([P, 2 * H], U8, name="w_raw%d" % a, align_bytes=64) for a in range(2)]
-        for a, words in enumerate((w1_words, w2_words)):
+        for a, words in enumerate((w2_words, w1_words)):
             nc.gpsimd.dma_start(w_raw[a][:].bitcast(I32), words[0].bitcast(I32))
         gain = sb.tile([P, PACK], F32, name="gain")
         nc.gpsimd.dma_start(gain[:], gs.rearrange("(p t) o -> p (t o)", t=PACK))
@@ -51,101 +51,108 @@ def tile_picked_thcifill_none_p_kernel(
         xs_run = sb.tile([P, T], U8, name="xs_run", align_bytes=64)
         nc.vector.memset(xs_run[:].bitcast(I32), 0)
         nc.scalar.dma_start(xs_run[0:P:8, :].bitcast(I32), x_rows)
+        ws_raw = sb.tile([P, 2 * H], U8, name="ws_raw", align_bytes=64)
+        nc.vector.memset(ws_raw[:].bitcast(I32), 0)
+        for a, scales in enumerate((w2_scales, w1_scales)):
+            nc.scalar.dma_start(ws_raw[0:P:8, a * H : (a + 1) * H].bitcast(I32), scales[0].bitcast(I32))
         xs = sb.tile([P, T], U8, name="xs", align_bytes=64)
         nc.vector.memset(xs[:].bitcast(I32), 0)
         for i in range(PACK):
-            nc.scalar.dma_start(xs[i:P:QUAD, :].bitcast(I32), x_rows[i:16:PACK, :])
-        ws_raw = [sb.tile([P, H], U8, name="ws_raw%d" % a, align_bytes=64) for a in range(2)]
-        for a, scales in enumerate((w1_scales, w2_scales)):
-            nc.vector.memset(ws_raw[a][:].bitcast(I32), 0)
-            rows = scales[0].bitcast(I32)
-            for i in range(PACK):
-                nc.scalar.dma_start(ws_raw[a][i:P:QUAD, :].bitcast(I32), rows[i:16:PACK, :])
+            nc.sync.dma_start(xs[i:P:QUAD, :].bitcast(I32), x_rows[i:16:PACK, :])
+        for dst, src in ((cand_l, cand), (n1_l, n1), (n2_l, n2)):
+            nc.sync.dma_start(dst[:], src)
 
-        hz_run = sb.tile([P, S], U8, name="hz_run", align_bytes=64)
+        hz_run = sb.tile([P, S], U8, name="hz_run", tag="hz_run", align_bytes=64)
         nc.vector.tensor_copy(hz_run[:], xs_run[:].indirect(hz_l[:]))
         hz_s = sb.tile([P, S], U8, name="hz_s", align_bytes=64)
         nc.vector.memset(hz_s[:].bitcast(I32), 0)
         for i in range(PACK):
-            nc.scalar.dma_start(hz_s[i:P:QUAD, :].bitcast(I32), hz_run[8 * i : P : QUAD, :].bitcast(I32))
+            nc.sync.dma_start(hz_s[i:P:QUAD, :].bitcast(I32), hz_run[8 * i : P : QUAD, :].bitcast(I32))
+        ws_dealt = sb.tile([P, 2 * H], U8, name="ws_dealt", tag="ws_dealt", align_bytes=64)
+        nc.vector.tensor_copy(
+            ws_dealt[:].rearrange("p (a t m) -> p a t m", a=2, t=PACK),
+            ws_raw[:].rearrange("p (a m t) -> p a t m", a=2, t=PACK),
+        )
+        ws = sb.tile([P, 2 * H], U8, name="ws", align_bytes=64)
+        nc.vector.memset(ws[:].bitcast(I32), 0)
+        for i in range(PACK):
+            nc.sync.dma_start(ws[i:P:QUAD, :].bitcast(I32), ws_dealt[8 * i : P : QUAD, :].bitcast(I32))
+        hz_w = sb.tile([P, S], U32, name="hz_w", align_bytes=64)
+        nc.vector.tensor_copy(hz_w[:], xw[:].indirect(hz_l[:]))
+        tok_w = sb.tile([P, S], U32, name="tok_w", align_bytes=64)
+        nc.vector.tensor_copy(tok_w[:], xw[:].indirect(offs_l[:]))
         tok_s = sb.tile([P, S], U8, name="tok_s", align_bytes=64)
         nc.vector.tensor_copy(tok_s[:], xs[:].indirect(offs_l[:]))
 
         w = [sb.tile([P, 2 * H], U8, name="w%d" % a, align_bytes=64) for a in range(2)]
-        ws = [sb.tile([P, H], U8, name="ws%d" % a, align_bytes=64) for a in range(2)]
         for a in range(2):
             nc.scalar.copy(
                 w[a][:].bitcast(U16).rearrange("p (t m) -> p t m", t=PACK),
                 w_raw[a][:].bitcast(U16).rearrange("p (m t) -> p t m", t=PACK),
             )
-            nc.vector.tensor_copy(
-                ws[a][:].rearrange("p (t m) -> p t m", t=PACK),
-                ws_raw[a][:].rearrange("p (m t) -> p t m", t=PACK),
-            )
 
-        tok_w = [sb.tile([P, HALF], U32, name="tok_w%d" % h, align_bytes=64) for h in range(2)]
-        hz_w = [sb.tile([P, HALF], U32, name="hz_w%d" % h, align_bytes=64) for h in range(2)]
-        z_rows = [sb.tile([P, PACK, HALF], BF16, name="z_rows%d" % h, align_bytes=64) for h in range(2)]
+        z_rows = []
         for h in range(2):
-            entries = slice(h * HALF // 16, (h + 1) * HALF // 16)
             cols = slice(h * HALF, (h + 1) * HALF)
-            nc.vector.tensor_copy(tok_w[h][:], xw[:].indirect(offs_l[:, entries]))
-            nc.vector.tensor_copy(hz_w[h][:], xw[:].indirect(hz_l[:, entries]))
             y = [psum.tile([P, HALF], F32, name="y%d%d" % (t, h), tag="bank%d%d" % (t, h)) for t in range(PACK)]
-            for a, (words, scales) in enumerate(((tok_w[h], tok_s), (hz_w[h], hz_s))):
+            for a, (words, scales) in enumerate(((hz_w, hz_s), (tok_w, tok_s))):
                 for t in range(PACK):
                     nc.tensor.matmul_mx(
                         out=y[t][:],
                         lhsT=w[a][:, 2 * P * t : 2 * P * (t + 1)].bitcast(FP4X4),
-                        lhsT_scale=ws[a][:, P * t : P * (t + 1)],
-                        rhs=words[:].bitcast(FP8X4),
+                        lhsT_scale=ws[:, a * H + P * t : a * H + P * (t + 1)],
+                        rhs=words[:, cols].bitcast(FP8X4),
                         rhs_scale=scales[:, cols],
                         start=(a == 0),
                         stop=(a == 1),
                     )
+            z_rows.append(sb.tile([P, PACK, HALF], BF16, name="z_rows%d" % h, align_bytes=64))
             for t in range(PACK):
                 nc.scalar.activation(z_rows[h][:, t, :], y[t][:], COPY, scale=gain[:, t : t + 1])
 
-        cand_s = sb.tile([P, C], U8, name="cand_s", align_bytes=64)
+        cand_s = sb.tile([P, C], U8, name="cand_s", tag="hz_run", align_bytes=64)
         nc.vector.tensor_copy(cand_s[:].rearrange("p (t m) -> p m t", t=PACK), xs[:].indirect(cand_l[:]))
-        cand_w = sb.tile([P, C], U32, name="cand_w", align_bytes=64)
+        cand_w = sb.tile([P, C], U32, name="cand_w", tag="ws_dealt", align_bytes=64)
         nc.vector.tensor_copy(cand_w[:].rearrange("p (t m) -> p m t", t=PACK), xw[:].indirect(cand_l[:]))
 
-        s = [sb.tile([P, S], F32, name="s%d" % t, align_bytes=64) for t in range(PACK)]
-        acc = {}
+        z_w = [sb.tile([P, HALF], U32, name="z_w%d" % h, align_bytes=64) for h in range(2)]
+        z_s = [sb.tile([P, HALF], U8, name="z_s%d" % h, align_bytes=64) for h in range(2)]
         for h in range(2):
             z = sb.tile([P, HALF, PACK], BF16, name="z%d" % h, align_bytes=64)
             nc.vector.tensor_copy(
                 z[:].rearrange("p (c i) t -> p c t i", i=PACK),
                 z_rows[h][:].rearrange("p t (c i) -> p c t i", i=PACK),
             )
-            z_w = sb.tile([P, HALF], U32, name="z_w%d" % h, align_bytes=64)
-            z_s = sb.tile([P, HALF], U8, name="z_s%d" % h, align_bytes=64)
-            nc.vector.quantize_mx(out=z_w[:].bitcast(FP8X4), scales=z_s[:], in_=z[:].rearrange("p j t -> p (j t)"))
-            for t in range(PACK):
-                acc[t, h] = psum.tile([P, HALF], F32, name="acc%d%d" % (t, h), tag="bank%d%d" % (t, h))
-                nc.tensor.matmul_mx(
-                    out=acc[t, h][:],
-                    lhsT=cand_w[:, P * t : P * (t + 1)].bitcast(FP8X4),
-                    lhsT_scale=cand_s[:, P * t : P * (t + 1)],
-                    rhs=z_w[:].bitcast(FP8X4),
-                    rhs_scale=z_s[:],
-                    start=True,
-                    stop=True,
-                )
+            nc.vector.quantize_mx(
+                out=z_w[h][:].bitcast(FP8X4), scales=z_s[h][:], in_=z[:].rearrange("p j t -> p (j t)")
+            )
+
+        def scores(dst, t, h):
+            nc.tensor.matmul_mx(
+                out=dst,
+                lhsT=cand_w[:, P * t : P * (t + 1)].bitcast(FP8X4),
+                lhsT_scale=cand_s[:, P * t : P * (t + 1)],
+                rhs=z_w[h][:].bitcast(FP8X4),
+                rhs_scale=z_s[h][:],
+                start=True,
+                stop=True,
+            )
 
         out_rows = out.rearrange("(p t) j -> p t j", t=PACK)
         for t in range(PACK):
+            s = sb.tile([P, S], F32, name="s%d" % t, align_bytes=64)
             for h in range(2):
-                nc.scalar.activation(s[t][:, h * HALF : (h + 1) * HALF], acc[t, h][:], COPY, scale=0.0625)
+                bank = psum.tile([P, HALF], F32, name="acc%d%d" % (t, h), tag="bank%d%d" % (t * (1 - h), h))
+                scores(bank[:], t, h)
+                nc.scalar.activation(s[:, h * HALF : (h + 1) * HALF], bank[:], COPY, scale=0.0625)
             pa = sb.tile([P, W], F32, name="pa%d" % t, align_bytes=64)
             pb = sb.tile([P, W], F32, name="pb%d" % t, align_bytes=64)
             ra = sb.tile([P, W], F32, name="ra%d" % t, align_bytes=64)
-            nc.scalar.activation(pb[:], s[t][:].indirect(n2_l[:]), COPY)
+            nc.scalar.activation(pb[:], s[:].indirect(n2_l[:]), COPY)
             if t == 0:
-                nc.vector.tensor_copy(pa[:], s[t][:].indirect(n1_l[:]))
+                nc.vector.tensor_copy(pa[:], s[:].indirect(n1_l[:]))
             else:
-                nc.scalar.activation(pa[:], s[t][:].indirect(n1_l[:]), COPY)
+                nc.scalar.activation(pa[:], s[:].indirect(n1_l[:]), COPY)
             nc.vector.tensor_tensor(ra[:], pa[:], pb[:], MAX)
-            nc.vector.tensor_copy(s[t][:].indirect(n1_l[:]), ra[:])
-            nc.sync.dma_start(out_rows[:, t, :], s[t][:])
+            nc.vector.tensor_copy(s[:].indirect(n1_l[:]), ra[:])
+            nc.sync.dma_start(out_rows[:, t, :], s[:])

@@ -36,11 +36,9 @@ def tile_picked_thcifill_none_p_kernel(
         cand_l = lists.tile([P, C // 16], U16, name="cand_l")
         n1_l = lists.tile([P, W // 16], U16, name="n1_l")
         n2_l = lists.tile([P, W // 16], U16, name="n2_l")
-        for dst, src in ((hz_l, hz), (offs_l, offs)):
+        for dst, src in ((hz_l, hz), (offs_l, offs), (cand_l, cand)):
             nc.sync.dma_start(dst[:], src)
 
-        xw = sb.tile([P, T], U32, name="xw", align_bytes=64)
-        nc.sync.dma_start(xw[:].bitcast(I32), x_words[0].rearrange("p n t -> p (n t)").bitcast(I32))
         w_raw = [sb.tile([P, 2 * H], U8, name="w_raw%d" % a, align_bytes=64) for a in range(2)]
         for a, words in enumerate((w2_words, w1_words)):
             nc.gpsimd.dma_start(w_raw[a][:].bitcast(I32), words[0].bitcast(I32))
@@ -51,36 +49,35 @@ def tile_picked_thcifill_none_p_kernel(
         xs_run = sb.tile([P, T], U8, name="xs_run", align_bytes=64)
         nc.vector.memset(xs_run[:].bitcast(I32), 0)
         nc.scalar.dma_start(xs_run[0:P:8, :].bitcast(I32), x_rows)
-        ws_raw = sb.tile([P, 2 * H], U8, name="ws_raw", align_bytes=64)
-        nc.vector.memset(ws_raw[:].bitcast(I32), 0)
-        for a, scales in enumerate((w2_scales, w1_scales)):
-            nc.scalar.dma_start(ws_raw[0:P:8, a * H : (a + 1) * H].bitcast(I32), scales[0].bitcast(I32))
         xs = sb.tile([P, T], U8, name="xs", align_bytes=64)
         nc.vector.memset(xs[:].bitcast(I32), 0)
         for i in range(PACK):
             nc.sync.dma_start(xs[i:P:QUAD, :].bitcast(I32), x_rows[i:16:PACK, :])
-        for dst, src in ((cand_l, cand), (n1_l, n1), (n2_l, n2)):
-            nc.sync.dma_start(dst[:], src)
+        ws_raw = sb.tile([P, H], U8, name="ws_raw", align_bytes=64)
+        nc.vector.memset(ws_raw[:].bitcast(I32), 0)
+        for a, scales in enumerate((w2_scales, w1_scales)):
+            nc.scalar.dma_start(ws_raw[4 * a : P : 8, :].bitcast(I32), scales[0].bitcast(I32))
+        xw = sb.tile([P, T], U32, name="xw", align_bytes=64)
+        nc.sync.dma_start(xw[:].bitcast(I32), x_words[0].rearrange("p n t -> p (n t)").bitcast(I32))
 
-        hz_run = sb.tile([P, S], U8, name="hz_run", tag="hz_run", align_bytes=64)
+        hz_run = sb.tile([P, S], U8, name="hz_run", align_bytes=64)
         nc.vector.tensor_copy(hz_run[:], xs_run[:].indirect(hz_l[:]))
         hz_s = sb.tile([P, S], U8, name="hz_s", align_bytes=64)
         nc.vector.memset(hz_s[:].bitcast(I32), 0)
         for i in range(PACK):
             nc.sync.dma_start(hz_s[i:P:QUAD, :].bitcast(I32), hz_run[8 * i : P : QUAD, :].bitcast(I32))
-        ws_dealt = sb.tile([P, 2 * H], U8, name="ws_dealt", tag="ws_dealt", align_bytes=64)
+        ws = [sb.tile([P, H], U8, name="ws%d" % a, align_bytes=64) for a in range(2)]
         nc.vector.tensor_copy(
-            ws_dealt[:].rearrange("p (a t m) -> p a t m", a=2, t=PACK),
-            ws_raw[:].rearrange("p (a m t) -> p a t m", a=2, t=PACK),
+            ws[0][:].rearrange("p (t m) -> p t m", t=PACK),
+            ws_raw[:].rearrange("p (m t) -> p t m", t=PACK),
         )
-        ws = sb.tile([P, 2 * H], U8, name="ws", align_bytes=64)
-        nc.vector.memset(ws[:].bitcast(I32), 0)
+        nc.vector.memset(ws[1][:].bitcast(I32), 0)
+        for i in range(1, PACK):
+            nc.sync.dma_start(ws[0][i:P:QUAD, :].bitcast(I32), ws[0][8 * i : P : QUAD, :].bitcast(I32))
         for i in range(PACK):
-            nc.sync.dma_start(ws[i:P:QUAD, :].bitcast(I32), ws_dealt[8 * i : P : QUAD, :].bitcast(I32))
-        hz_w = sb.tile([P, S], U32, name="hz_w", align_bytes=64)
-        nc.vector.tensor_copy(hz_w[:], xw[:].indirect(hz_l[:]))
-        tok_w = sb.tile([P, S], U32, name="tok_w", align_bytes=64)
-        nc.vector.tensor_copy(tok_w[:], xw[:].indirect(offs_l[:]))
+            nc.sync.dma_start(ws[1][i:P:QUAD, :].bitcast(I32), ws[0][8 * i + 4 : P : QUAD, :].bitcast(I32))
+        for dst, src in ((n1_l, n1), (n2_l, n2)):
+            nc.sync.dma_start(dst[:], src)
         tok_s = sb.tile([P, S], U8, name="tok_s", align_bytes=64)
         nc.vector.tensor_copy(tok_s[:], xs[:].indirect(offs_l[:]))
 
@@ -94,14 +91,19 @@ def tile_picked_thcifill_none_p_kernel(
         z_rows = []
         for h in range(2):
             cols = slice(h * HALF, (h + 1) * HALF)
-            y = [psum.tile([P, HALF], F32, name="y%d%d" % (t, h), tag="bank%d%d" % (t, h)) for t in range(PACK)]
-            for a, (words, scales) in enumerate(((hz_w, hz_s), (tok_w, tok_s))):
-                for t in range(PACK):
+            entries = slice(h * HALF // 16, (h + 1) * HALF // 16)
+            hz_w = sb.tile([P, HALF], U32, name="hz_w%d" % h, tag="hz_w%d" % h, align_bytes=64)
+            nc.vector.tensor_copy(hz_w[:], xw[:].indirect(hz_l[:, entries]))
+            tok_w = sb.tile([P, HALF], U32, name="tok_w%d" % h, align_bytes=64)
+            nc.vector.tensor_copy(tok_w[:], xw[:].indirect(offs_l[:, entries]))
+            y = [psum.tile([P, HALF], F32, name="y%d%d" % (t, h), tag="y%d" % t) for t in range(PACK)]
+            for t in range(PACK):
+                for a, (words, scales) in enumerate(((hz_w, hz_s), (tok_w, tok_s))):
                     nc.tensor.matmul_mx(
                         out=y[t][:],
                         lhsT=w[a][:, 2 * P * t : 2 * P * (t + 1)].bitcast(FP4X4),
-                        lhsT_scale=ws[:, a * H + P * t : a * H + P * (t + 1)],
-                        rhs=words[:, cols].bitcast(FP8X4),
+                        lhsT_scale=ws[a][:, P * t : P * (t + 1)],
+                        rhs=words[:].bitcast(FP8X4),
                         rhs_scale=scales[:, cols],
                         start=(a == 0),
                         stop=(a == 1),
@@ -110,19 +112,24 @@ def tile_picked_thcifill_none_p_kernel(
             for t in range(PACK):
                 nc.scalar.activation(z_rows[h][:, t, :], y[t][:], COPY, scale=gain[:, t : t + 1])
 
-        cand_s = sb.tile([P, C], U8, name="cand_s", tag="hz_run", align_bytes=64)
-        nc.vector.tensor_copy(cand_s[:].rearrange("p (t m) -> p m t", t=PACK), xs[:].indirect(cand_l[:]))
-        cand_w = sb.tile([P, C], U32, name="cand_w", tag="ws_dealt", align_bytes=64)
+        cand_w = sb.tile([P, C], U32, name="cand_w", align_bytes=64)
         nc.vector.tensor_copy(cand_w[:].rearrange("p (t m) -> p m t", t=PACK), xw[:].indirect(cand_l[:]))
+        cand_s = sb.tile([P, C], U8, name="cand_s", tag="hz_w0", align_bytes=64)
+        nc.vector.tensor_copy(cand_s[:].rearrange("p (t m) -> p m t", t=PACK), xs[:].indirect(cand_l[:]))
 
         z_w = [sb.tile([P, HALF], U32, name="z_w%d" % h, align_bytes=64) for h in range(2)]
         z_s = [sb.tile([P, HALF], U8, name="z_s%d" % h, align_bytes=64) for h in range(2)]
         for h in range(2):
             z = sb.tile([P, HALF, PACK], BF16, name="z%d" % h, align_bytes=64)
-            nc.vector.tensor_copy(
-                z[:].rearrange("p (c i) t -> p c t i", i=PACK),
-                z_rows[h][:].rearrange("p t (c i) -> p c t i", i=PACK),
-            )
+            if h == 0:
+                shares = ((nc.vector.tensor_copy, slice(0, HALF)),)
+            else:
+                shares = ((nc.scalar.copy, slice(0, HALF // 2)), (nc.vector.tensor_copy, slice(HALF // 2, HALF)))
+            for copy, cols in shares:
+                copy(
+                    z[:, cols, :].rearrange("p (c i) t -> p c t i", i=PACK),
+                    z_rows[h][:, :, cols].rearrange("p t (c i) -> p c t i", i=PACK),
+                )
             nc.vector.quantize_mx(
                 out=z_w[h][:].bitcast(FP8X4), scales=z_s[h][:], in_=z[:].rearrange("p j t -> p (j t)")
             )
@@ -142,7 +149,7 @@ def tile_picked_thcifill_none_p_kernel(
         for t in range(PACK):
             s = sb.tile([P, S], F32, name="s%d" % t, align_bytes=64)
             for h in range(2):
-                bank = psum.tile([P, HALF], F32, name="acc%d%d" % (t, h), tag="bank%d%d" % (t * (1 - h), h))
+                bank = psum.tile([P, HALF], F32, name="acc%d%d" % (t, h), tag=("first%d" % t, "y0")[h])
                 scores(bank[:], t, h)
                 nc.scalar.activation(s[:, h * HALF : (h + 1) * HALF], bank[:], COPY, scale=0.0625)
             pa = sb.tile([P, W], F32, name="pa%d" % t, align_bytes=64)

from contextlib import ExitStack

import concourse.mybir as mybir

K, T, S, H, C, W = 512, 2048, 512, 512, 512, 256
FLOPS = 3 * 2 * 512 * 512 * 512

F32 = mybir.dt.float32
BF16 = mybir.dt.bfloat16
I32 = mybir.dt.int32
U32 = mybir.dt.uint32
U16 = mybir.dt.uint16
U8 = mybir.dt.uint8
FP8X4 = mybir.dt.float8_e4m3fn_x4
FP4X4 = mybir.dt.float4_e2m1fn_x4
COPY = mybir.ActivationFunctionType.Copy
MAX = mybir.AluOpType.max

P = 128
PACK = 4
HALF = S // 2
QUAD = 32


def tile_picked_thcifill_none_p_kernel(
    tc, x_words, x_scales, w1_words, w1_scales, w2_words, w2_scales, gs, offs, hz, cand, n1, n2, out
):
    nc = tc.nc
    with ExitStack() as ctx:
        lists = ctx.enter_context(tc.tile_pool(name="lists", bufs=1))
        sb = ctx.enter_context(tc.tile_pool(name="sb", bufs=1))
        psum = ctx.enter_context(tc.psum_pool(name="psum", bufs=1))

        hz_l = lists.tile([P, S // 16], U16, name="hz_l")
        offs_l = lists.tile([P, S // 16], U16, name="offs_l")
        cand_l = lists.tile([P, C // 16], U16, name="cand_l")
        n1_l = lists.tile([P, W // 16], U16, name="n1_l")
        n2_l = lists.tile([P, W // 16], U16, name="n2_l")
        for dst, src in ((hz_l, hz), (offs_l, offs), (cand_l, cand)):
            nc.sync.dma_start(dst[:], src)

        w_raw = [sb.tile([P, 2 * H], U8, name="w_raw%d" % a, align_bytes=64) for a in range(2)]
        for a, words in enumerate((w2_words, w1_words)):
            nc.gpsimd.dma_start(w_raw[a][:].bitcast(I32), words[0].bitcast(I32))
        gain = sb.tile([P, PACK], F32, name="gain")
        nc.gpsimd.dma_start(gain[:], gs.rearrange("(p t) o -> p (t o)", t=PACK))

        x_rows = x_scales[0].bitcast(I32)
        xs_run = sb.tile([P, T], U8, name="xs_run", align_bytes=64)
        nc.vector.memset(xs_run[:].bitcast(I32), 0)
        nc.scalar.dma_start(xs_run[0:P:8, :].bitcast(I32), x_rows)
        xs = sb.tile([P, T], U8, name="xs", align_bytes=64)
        nc.vector.memset(xs[:].bitcast(I32), 0)
        for i in range(PACK):
            nc.sync.dma_start(xs[i:P:QUAD, :].bitcast(I32), x_rows[i:16:PACK, :])
        ws_raw = sb.tile([P, H], U8, name="ws_raw", align_bytes=64)
        nc.vector.memset(ws_raw[:].bitcast(I32), 0)
        for a, scales in enumerate((w2_scales, w1_scales)):
            nc.scalar.dma_start(ws_raw[4 * a : P : 8, :].bitcast(I32), scales[0].bitcast(I32))
        xw = sb.tile([P, T], U32, name="xw", align_bytes=64)
        nc.sync.dma_start(xw[:].bitcast(I32), x_words[0].rearrange("p n t -> p (n t)").bitcast(I32))

        hz_run = sb.tile([P, S], U8, name="hz_run", align_bytes=64)
        nc.vector.tensor_copy(hz_run[:], xs_run[:].indirect(hz_l[:]))
        hz_s = sb.tile([P, S], U8, name="hz_s", align_bytes=64)
        nc.vector.memset(hz_s[:].bitcast(I32), 0)
        for i in range(PACK):
            nc.sync.dma_start(hz_s[i:P:QUAD, :].bitcast(I32), hz_run[8 * i : P : QUAD, :].bitcast(I32))
        ws = [sb.tile([P, H], U8, name="ws%d" % a, align_bytes=64) for a in range(2)]
        nc.vector.tensor_copy(
            ws[0][:].rearrange("p (t m) -> p t m", t=PACK),
            ws_raw[:].rearrange("p (m t) -> p t m", t=PACK),
        )
        nc.vector.memset(ws[1][:].bitcast(I32), 0)
        for i in range(1, PACK):
            nc.sync.dma_start(ws[0][i:P:QUAD, :].bitcast(I32), ws[0][8 * i : P : QUAD, :].bitcast(I32))
        for i in range(PACK):
            nc.sync.dma_start(ws[1][i:P:QUAD, :].bitcast(I32), ws[0][8 * i + 4 : P : QUAD, :].bitcast(I32))
        for dst, src in ((n1_l, n1), (n2_l, n2)):
            nc.sync.dma_start(dst[:], src)
        tok_s = sb.tile([P, S], U8, name="tok_s", align_bytes=64)
        nc.vector.tensor_copy(tok_s[:], xs[:].indirect(offs_l[:]))

        w = [sb.tile([P, 2 * H], U8, name="w%d" % a, align_bytes=64) for a in range(2)]
        for a in range(2):
            nc.scalar.copy(
                w[a][:].bitcast(U16).rearrange("p (t m) -> p t m", t=PACK),
                w_raw[a][:].bitcast(U16).rearrange("p (m t) -> p t m", t=PACK),
            )

        z_rows = []
        for h in range(2):
            cols = slice(h * HALF, (h + 1) * HALF)
            entries = slice(h * HALF // 16, (h + 1) * HALF // 16)
            hz_w = sb.tile([P, HALF], U32, name="hz_w%d" % h, tag="hz_w%d" % h, align_bytes=64)
            nc.vector.tensor_copy(hz_w[:], xw[:].indirect(hz_l[:, entries]))
            tok_w = sb.tile([P, HALF], U32, name="tok_w%d" % h, align_bytes=64)
            nc.vector.tensor_copy(tok_w[:], xw[:].indirect(offs_l[:, entries]))
            y = [psum.tile([P, HALF], F32, name="y%d%d" % (t, h), tag="y%d" % t) for t in range(PACK)]
            for t in range(PACK):
                for a, (words, scales) in enumerate(((hz_w, hz_s), (tok_w, tok_s))):
                    nc.tensor.matmul_mx(
                        out=y[t][:],
                        lhsT=w[a][:, 2 * P * t : 2 * P * (t + 1)].bitcast(FP4X4),
                        lhsT_scale=ws[a][:, P * t : P * (t + 1)],
                        rhs=words[:].bitcast(FP8X4),
                        rhs_scale=scales[:, cols],
                        start=(a == 0),
                        stop=(a == 1),
                    )
            z_rows.append(sb.tile([P, PACK, HALF], BF16, name="z_rows%d" % h, align_bytes=64))
            for t in range(PACK):
                nc.scalar.activation(z_rows[h][:, t, :], y[t][:], COPY, scale=gain[:, t : t + 1])

        cand_w = sb.tile([P, C], U32, name="cand_w", align_bytes=64)
        nc.vector.tensor_copy(cand_w[:].rearrange("p (t m) -> p m t", t=PACK), xw[:].indirect(cand_l[:]))
        cand_s = sb.tile([P, C], U8, name="cand_s", tag="hz_w0", align_bytes=64)
        nc.vector.tensor_copy(cand_s[:].rearrange("p (t m) -> p m t", t=PACK), xs[:].indirect(cand_l[:]))

        z_w = [sb.tile([P, HALF], U32, name="z_w%d" % h, align_bytes=64) for h in range(2)]
        z_s = [sb.tile([P, HALF], U8, name="z_s%d" % h, align_bytes=64) for h in range(2)]
        for h in range(2):
            z = sb.tile([P, HALF, PACK], BF16, name="z%d" % h, align_bytes=64)
            if h == 0:
                shares = ((nc.vector.tensor_copy, slice(0, HALF)),)
            else:
                shares = ((nc.scalar.copy, slice(0, HALF // 2)), (nc.vector.tensor_copy, slice(HALF // 2, HALF)))
            for copy, cols in shares:
                copy(
                    z[:, cols, :].rearrange("p (c i) t -> p c t i", i=PACK),
                    z_rows[h][:, :, cols].rearrange("p t (c i) -> p c t i", i=PACK),
                )
            nc.vector.quantize_mx(
                out=z_w[h][:].bitcast(FP8X4), scales=z_s[h][:], in_=z[:].rearrange("p j t -> p (j t)")
            )

        def scores(dst, t, h):
            nc.tensor.matmul_mx(
                out=dst,
                lhsT=cand_w[:, P * t : P * (t + 1)].bitcast(FP8X4),
                lhsT_scale=cand_s[:, P * t : P * (t + 1)],
                rhs=z_w[h][:].bitcast(FP8X4),
                rhs_scale=z_s[h][:],
                start=True,
                stop=True,
            )

        out_rows = out.rearrange("(p t) j -> p t j", t=PACK)
        for t in range(PACK):
            s = sb.tile([P, S], F32, name="s%d" % t, align_bytes=64)
            for h in range(2):
                bank = psum.tile([P, HALF], F32, name="acc%d%d" % (t, h), tag=("first%d" % t, "y0")[h])
                scores(bank[:], t, h)
                nc.scalar.activation(s[:, h * HALF : (h + 1) * HALF], bank[:], COPY, scale=0.0625)
            pa = sb.tile([P, W], F32, name="pa%d" % t, align_bytes=64)
            pb = sb.tile([P, W], F32, name="pb%d" % t, align_bytes=64)
            ra = sb.tile([P, W], F32, name="ra%d" % t, align_bytes=64)
            nc.scalar.activation(pb[:], s[:].indirect(n2_l[:]), COPY)
            if t == 0:
                nc.vector.tensor_copy(pa[:], s[:].indirect(n1_l[:]))
            else:
                nc.scalar.activation(pa[:], s[:].indirect(n1_l[:]), COPY)
            nc.vector.tensor_tensor(ra[:], pa[:], pb[:], MAX)
            nc.vector.tensor_copy(s[:].indirect(n1_l[:]), ra[:])
            nc.sync.dma_start(out_rows[:, t, :], s[:])
